import numpy as np
import ml_dtypes


def mxq(x, axis, fmt="e4m3"):
    dtype, down = {"e4m3": (ml_dtypes.float8_e4m3fn, 7), "e5m2": (ml_dtypes.float8_e5m2, 14)}[fmt]
    v = np.moveaxis(np.asarray(x, np.float32).astype(ml_dtypes.bfloat16).astype(np.float64), axis, -1)
    blocks = v.reshape(v.shape[:-1] + (-1, 32))
    amax = np.abs(blocks).max(-1, keepdims=True)
    byte = np.maximum(np.where(amax > 0, np.frexp(amax)[1] - 1 + 127, 0) - down, 1)
    scale = np.exp2(byte - 127.0)
    codes = (blocks / scale).astype(np.float32).astype(dtype).astype(np.float64)
    return np.moveaxis((codes * scale).reshape(v.shape), -1, axis)


WIDE = False


def mx_kscale(k):
    if not WIDE:
        return np.ones(k)
    levels = np.array([10, -10, 5, -5, 0])
    if k % 512:
        return np.exp2(np.random.permutation(np.resize(levels, k // 32))).repeat(32)
    a = np.empty((k // 512, 16))
    for p in range(k // 512):
        a[p, :8] = np.random.permutation(np.resize(levels, 8))
        for g in range(8):
            far = levels[np.abs(levels - a[p, g]) >= 10]
            a[p, g + 8] = far[np.random.randint(len(far))]
    return np.exp2(a.ravel()).repeat(32)


def f64(x):
    return np.asarray(x).astype(np.float64)


def striped(idx):
    return np.tile(idx.reshape(-1, 16).T, (8, 1)).astype(np.uint16)


def unstriped(offs):
    return offs[:16].T.reshape(-1).astype(np.int64)


E2M1 = np.array([0.0, 0.5, 1.0, 1.5, 2.0, 3.0, 4.0, 6.0, -0.0, -0.5, -1.0, -1.5, -2.0, -3.0, -4.0, -6.0])


def pack_weight(w, fmt):
    k, n = w.shape
    w = f64(np.asarray(w, np.float32).astype(ml_dtypes.bfloat16)).reshape(k // 32, 32, n)
    amax = np.abs(w).max(1)
    if fmt == "e4m3":
        byte = np.frexp(amax)[1] - 1 + 127 - 7
    else:
        mant, ex = np.frexp(amax / 6.0)
        byte = np.where(mant > 0.5, ex, ex - 1) + 127
    byte = np.clip(np.where(amax > 0, byte, 1), 1, 254)
    scaled = (w * np.exp2(127.0 - byte)[:, None, :]).reshape(k, n).astype(np.float32)
    by_word = np.ascontiguousarray(scaled.reshape(k // 512, 128, 4, n).transpose(0, 1, 3, 2))
    if fmt == "e4m3":
        words = by_word.astype(ml_dtypes.float8_e4m3fn).view(np.uint8)
    else:
        c = by_word.astype(ml_dtypes.float4_e2m1fn).view(np.uint8) & 0xF
        words = (c[..., 0::2] | (c[..., 1::2] << 4)).reshape(k // 512, 128, 2 * n)
    return np.ascontiguousarray(words), np.ascontiguousarray(byte.astype(np.uint8).reshape(k // 512, 16, n))


def unpack_weight(words, scales, fmt):
    g, _, n = scales.shape
    words = np.ascontiguousarray(words).reshape(g, 128, n, -1)
    if fmt == "e4m3":
        vals = words.view(ml_dtypes.float8_e4m3fn).astype(np.float64)
    else:
        nib = np.empty((g, 128, n, 4), np.uint8)
        nib[..., 0::2] = words & 0xF
        nib[..., 1::2] = words >> 4
        vals = E2M1[nib]
    vals = vals * np.repeat(np.exp2(scales.astype(np.float64) - 127.0), 8, axis=1)[..., None]
    return vals.transpose(0, 1, 3, 2).reshape(g * 512, n)


def gelu(v):
    return 0.5 * v * (1.0 + np.tanh(np.sqrt(2.0 / np.pi) * (v + 0.044715 * v**3)))


def striped8(idx):
    return np.concatenate([v.reshape(-1, 16).T for v in idx]).astype(np.uint16)


def unstriped8(offs):
    return np.stack([offs[16 * g:16 * g + 16].T.reshape(-1) for g in range(8)]).astype(np.int64)


def runs(v, idx8):
    k = np.arange(v.shape[0])
    return v[k[:, None], idx8[k % 512 // 64]]


K, T, S, P, H, N = 512, 2048, 1024, 512, 1024, 384


def setup_inputs():
    n = np.random.standard_normal
    s = mx_kscale(K)[:, None]
    u = mx_kscale(H)[:, None]
    d = {}
    d["tab_words"], d["tab_scales"] = pack_weight(n((K, T)) * s, "e4m3")
    d["offs"] = striped8(np.stack([np.random.permutation(T)[:S] for _ in range(8)]))
    d["pos1"] = striped(np.random.permutation(S)[:P])
    d["pos2"] = striped(np.random.permutation(S)[:P])
    d["w1_words"], d["w1_scales"] = pack_weight(n((K, H)) / K**0.5 / s * u.T, "e2m1")
    d["w2"] = (n((K, H)) / K**0.5 / s * u.T).astype(np.float32)
    d["w3"] = (n((K, H)) / K**0.5 / s * u.T).astype(np.float32)
    d["w4_words"], d["w4_scales"] = pack_weight(2.0 * n((H, N)) / H**0.5 / u, "e4m3")
    d["side"] = np.exp(0.4 * n(H)).astype(np.float32)
    d["base"] = (0.35 * np.exp(0.5 * n(N))).astype(np.float32)
    return d


def reference(tab_words, tab_scales, offs, pos1, pos2, w1_words, w1_scales, w2, w3, w4_words, w4_scales, side, base):
    v = runs(unpack_weight(tab_words, tab_scales, "e4m3"), unstriped8(offs))
    a = unpack_weight(w1_words, w1_scales, "e2m1").T @ v
    b = mxq(f64(w2), 0, "e4m3").T @ v
    e = mxq(f64(w3), 0, "e4m3").T @ v
    h = np.maximum(np.maximum(a, b), e)
    z = h[:, unstriped(pos1)] - f64(side)[:, None] * h[:, unstriped(pos2)]
    y = unpack_weight(w4_words, w4_scales, "e4m3").T @ mxq(z, 0, "e4m3")
    return np.sqrt(np.abs(y) + f64(base)[:, None])

@@ -1,0 +1,326 @@
+from contextlib import ExitStack
+
+import concourse.mybir as mybir
+from concourse.masks import make_identity
+
+K, T, S, M, H, N = 512, 2048, 1024, 512, 1024, 384
+FLOPS = 2 * (3 * K * H * S + H * N * M)
+
+F32 = mybir.dt.float32
+BF16 = mybir.dt.bfloat16
+I32 = mybir.dt.int32
+U32 = mybir.dt.uint32
+U16 = mybir.dt.uint16
+U8 = mybir.dt.uint8
+FP8X4 = mybir.dt.float8_e4m3fn_x4
+FP4X4 = mybir.dt.float4_e2m1fn_x4
+ALU = mybir.AluOpType
+ACT = mybir.ActivationFunctionType
+
+P = 128
+BANK = 512
+R_TILES = H // P
+N_TILES = N // P
+TAIL_TILES = 4
+M_CHUNKS = ((0, 256), (256, 128), (384, 128))
+CHUNKS = ((0, 2, "a"), (2, 2, "b"), (4, 4, "a"))
+
+
+def tile_list_sleeper_support_rating_kernel(
+    tc, tab_words, tab_scales, offs, pos1, pos2, w1_words, w1_scales, w2, w3, w4_words, w4_scales, side, base, out
+):
+    nc = tc.nc
+    with ExitStack() as ctx:
+        held = ctx.enter_context(tc.tile_pool(name="held", bufs=1))
+        stage = ctx.enter_context(tc.tile_pool(name="stage", bufs=1))
+        ring2 = ctx.enter_context(tc.tile_pool(name="ring2", bufs=2))
+        ring3 = ctx.enter_context(tc.tile_pool(name="ring3", bufs=3))
+        ring4 = ctx.enter_context(tc.tile_pool(name="ring4", bufs=4))
+        psum = ctx.enter_context(tc.psum_pool(name="psum", bufs=1))
+
+        offs_t = held.tile([P, S // 16], U16, name="offs_t")
+        pos1_t = held.tile([P, M // 16], U16, name="pos1_t")
+        pos2_t = held.tile([P, M // 16], U16, name="pos2_t")
+        table_words = held.tile([P, T], U32, name="table_words", align_bytes=64)
+        table_bytes = stage.tile([P, T], U8, name="table_bytes", tag="b", align_bytes=64)
+        picked_bytes = held.tile([P, S], U8, name="picked_bytes", align_bytes=64)
+        v_scales = held.tile([P, S], U8, name="v_scales", align_bytes=64)
+        v_words = [held.tile([P, BANK], U32, name="v_words%d" % half, align_bytes=64) for half in range(2)]
+        w1_codes = held.tile([P, 2 * H], U8, name="w1_codes", align_bytes=64)
+        w1_plane = held.tile([P, H], U8, name="w1_plane", align_bytes=64)
+        w4_plane = held.tile([P, 2, N], U8, name="w4_plane", align_bytes=64)
+        rows = held.tile([P, P], F32, name="rows")
+        identity = held.tile([P, P], F32, name="identity")
+        neg_side = held.tile([P, R_TILES], F32, name="neg_side")
+        base_col = held.tile([P, N_TILES], F32, name="base_col")
+
+        nc.gpsimd.memset(table_bytes[:].bitcast(I32), 0)
+        nc.vector.memset(w1_plane[:].bitcast(I32), 0)
+        nc.vector.memset(rows[:], 0.0)
+        nc.vector.memset(v_scales[:].bitcast(I32), 0)
+        nc.vector.memset(w4_plane[:].rearrange("p a n -> p (a n)").bitcast(I32), 0)
+        nc.sync.dma_start(offs_t[:], offs)
+        nc.sync.dma_start(pos2_t[:], pos2)
+        nc.sync.dma_start(pos1_t[:], pos1)
+        nc.sync.dma_start(table_words[:].bitcast(I32), tab_words[0].rearrange("p t i -> p (t i)").bitcast(I32))
+        nc.scalar.dma_start(table_bytes[0:P:8, :].bitcast(I32), tab_scales[0].bitcast(I32))
+        for d in range(4):
+            queue = nc.gpsimd if d < 3 else nc.scalar
+            queue.dma_start(
+                w1_plane[32 * d : 32 * d + 4, :].bitcast(I32), w1_scales[0, 4 * d : 4 * d + 4, :].bitcast(I32)
+            )
+        nc.sync.dma_start(w1_codes[:].bitcast(I32), w1_words[0].bitcast(I32))
+
+        raw = {}
+
+        def load_chunk(first, count, tag):
+            cols = slice(first * P, (first + count) * P)
+            chunk = stage.tile([P, 2, 4, count * P], F32, name="chunk", tag=tag, align_bytes=64)
+            for slot, w in enumerate((w2, w3)):
+                nc.sync.dma_start(chunk[:, slot, :, :], w[:, cols].rearrange("(p j) c -> p j c", j=4))
+                for i in range(count):
+                    raw[(slot, first + i)] = chunk[:, slot, :, i * P : (i + 1) * P]
+
+        load_chunk(*CHUNKS[0])
+
+        make_identity(nc, identity[:])
+        nc.gpsimd.dma_start(rows[0:R_TILES, :], side.rearrange("(i p) -> i p", p=P))
+        nc.gpsimd.dma_start(rows[R_TILES : R_TILES + N_TILES, :], base.rearrange("(i p) -> i p", p=P))
+        for d in range(4):
+            nc.gpsimd.dma_start(
+                w4_plane[32 * d : 32 * d + 4, :, :].bitcast(I32),
+                w4_scales[:, 4 * d : 4 * d + 4, :].rearrange("a q n -> q a n").bitcast(I32),
+            )
+
+        nc.vector.tensor_copy(picked_bytes[:], table_bytes[:].indirect(offs_t[:]))
+        for r in range(4):
+            queue = nc.scalar if r % 2 else nc.sync
+            queue.dma_start(v_scales[r:P:32, :].bitcast(I32), picked_bytes[8 * r : P : 32, :].bitcast(I32))
+        load_chunk(*CHUNKS[1])
+        for half in range(2):
+            nc.vector.tensor_copy(v_words[half][:], table_words[:].indirect(offs_t[:, 32 * half : 32 * half + 32]))
+
+        quantised = {}
+
+        def prepare(i):
+            grouped = ring2.tile([P, 2, P, 4], BF16, name="grouped", align_bytes=64)
+            for slot in range(2):
+                nc.scalar.copy(
+                    grouped[:, slot, :, :].rearrange("p (c i) t -> p c t i", i=4),
+                    raw[(slot, i)].rearrange("p t (c i) -> p c t i", i=4),
+                )
+            codes = ring3.tile([P, 2 * P], U32, name="w_codes", align_bytes=64)
+            scales = ring3.tile([P, 2 * P], U8, name="w_scales", align_bytes=64)
+            parts = 2 if i == 0 else 1
+            width = 2 * P // parts
+            flat = grouped[:].rearrange("p s c t -> p (s c t)")
+            for part in range(parts):
+                cols = slice(part * width, (part + 1) * width)
+                nc.vector.quantize_mx(
+                    out=codes[:, cols].bitcast(FP8X4),
+                    scales=scales[:, cols],
+                    in_=flat[:, 4 * part * width : 4 * (part + 1) * width],
+                )
+            quantised[i] = (codes, scales)
+
+        sums = {}
+
+        def multiply(i, half):
+            codes, scales = quantised[i]
+            moving = v_words[half][:].bitcast(FP8X4)
+            moving_scales = v_scales[:, half * BANK : (half + 1) * BANK]
+            banks = [psum.tile([P, BANK], F32, name="sums", tag="bank%d" % (2 * k + half)) for k in range(3)]
+            nc.tensor.matmul_mx(
+                out=banks[0][:],
+                lhsT=w1_codes[:, 2 * P * i : 2 * P * (i + 1)].bitcast(FP4X4),
+                lhsT_scale=w1_plane[:, P * i : P * (i + 1)],
+                rhs=moving,
+                rhs_scale=moving_scales,
+                start=True,
+                stop=True,
+            )
+            for slot in range(2):
+                nc.tensor.matmul_mx(
+                    out=banks[1 + slot][:],
+                    lhsT=codes[:, slot * P : (slot + 1) * P].bitcast(FP8X4),
+                    lhsT_scale=scales[:, slot * P : (slot + 1) * P],
+                    rhs=moving,
+                    rhs_scale=moving_scales,
+                    start=True,
+                    stop=True,
+                )
+            first = ring3.tile([P, BANK], F32, name="first")
+            nc.scalar.copy(first[:], banks[0][:])
+            sums[(i, half)] = (first, banks[1], banks[2])
+
+        def max_first(i, half):
+            first, second, third = sums[(i, half)]
+            pair = ring2.tile([P, BANK], F32, name="pair", tag="pair")
+            nc.vector.tensor_tensor(pair[:], second[:], first[:], ALU.max)
+            sums[(i, half)] = (pair, third)
+
+        h_tiles = {}
+
+        def max_second(i, half):
+            pair, third = sums[(i, half)]
+            if half == 0:
+                h_tiles[i] = ring4.tile([P, S], F32, name="h", bufs=5)
+            nc.vector.tensor_tensor(h_tiles[i][:, half * BANK : (half + 1) * BANK], third[:], pair[:], ALU.max)
+
+        def pick_side(i, m0, width, picked):
+            nc.vector.tensor_copy(picked, h_tiles[i][:].indirect(pos2_t[:, m0 // 16 : (m0 + width) // 16]))
+            weighted = ring3.tile([P, width], F32, name="weighted", tag="weighted")
+            nc.scalar.activation(weighted[:], picked, ACT.Copy, scale=neg_side[:, i : i + 1])
+            return weighted
+
+        z_rows = {}
+
+        def pick_supine(i, m0, width, weighted, picked, bank):
+            nc.vector.tensor_copy(picked, h_tiles[i][:].indirect(pos1_t[:, m0 // 16 : (m0 + width) // 16]))
+            blocks = width // P
+            turned = psum.tile([P, blocks, P], F32, name="turned", tag=bank)
+            for mt in range(blocks):
+                cols = slice(mt * P, (mt + 1) * P)
+                nc.tensor.matmul(
+                    turned[:, mt, :], weighted[:, cols], identity[:], start=True, stop=False, is_transpose=True
+                )
+                nc.tensor.matmul(
+                    turned[:, mt, :], picked[:, cols], identity[:], start=False, stop=True, is_transpose=True
+                )
+            b, quarter = divmod(i, 4)
+            if (b, m0) not in z_rows:
+                z_rows[(b, m0)] = held.tile([P, blocks, 2, 2 * P], BF16, name="z_rows%d_%d" % (b, m0), align_bytes=64)
+            nc.scalar.copy(
+                z_rows[(b, m0)][:, :, :, 64 * quarter : 64 * (quarter + 1)].rearrange("m t u (q e) -> m t u q e", e=2),
+                turned[:].rearrange("m t (q u e) -> m t u q e", u=2, e=2),
+            )
+
+        z_quantised = {}
+
+        def turn_back(b, c0, cw, on_vector):
+            words = z_rows[(b, c0)][:].rearrange("m t u w -> m (t u w)").bitcast(F32)
+            grouped = held.tile([P, cw * 4], BF16, name="z_grouped%d_%d" % (b, c0), align_bytes=64)
+            blocks = min(2, cw // P)
+            for first_block in range(0, cw // P, blocks):
+                back = psum.tile([P, blocks, 2, P], F32, name="back", tag="bank7")
+                for mt in range(blocks):
+                    for u in range(2):
+                        at = (2 * (first_block + mt) + u) * P
+                        nc.tensor.transpose(back[:, mt, u, :], words[:, at : at + P], identity[:])
+                target = grouped[:, 4 * P * first_block : 4 * P * (first_block + blocks)].bitcast(F32)
+                target = target.rearrange("p (t m u) -> p t m u", t=blocks, u=2)
+                source = back[:].rearrange("p t u m -> p t m u")
+                if on_vector:
+                    nc.vector.tensor_copy(target, source)
+                else:
+                    nc.scalar.copy(target, source)
+            z_quantised[(b, c0)] = grouped
+
+        def quantise_z(b, c0, cw):
+            grouped = z_quantised[(b, c0)]
+            codes = held.tile([P, cw], U32, name="z_codes%d_%d" % (b, c0), align_bytes=64)
+            scales = held.tile([P, cw], U8, name="z_scales%d_%d" % (b, c0), align_bytes=64)
+            nc.vector.quantize_mx(out=codes[:].bitcast(FP8X4), scales=scales[:], in_=grouped[:])
+            z_quantised[(b, c0)] = (codes, scales)
+
+        prepare(0)
+        multiply(0, 0)
+        multiply(0, 1)
+        prepare(1)
+        load_chunk(*CHUNKS[2])
+
+        columns = psum.tile([P, P], F32, name="columns", tag="bank6")
+        nc.tensor.transpose(columns[:], rows[:], identity[:])
+        nc.scalar.activation(neg_side[:], columns[:, 0:R_TILES], ACT.Copy, scale=-1.0)
+        nc.scalar.copy(base_col[:], columns[:, R_TILES : R_TILES + N_TILES])
+
+        w4_codes = None
+        whole_tiles = R_TILES - TAIL_TILES
+        for i in range(R_TILES):
+            picks = i > 0
+            width = M if i <= whole_tiles else M_CHUNKS[0][1]
+            max_first(i, 0)
+            if picks:
+                picked = ring2.tile([P, 2, width], F32, name="picked", tag="picked")
+                weighted = pick_side(i - 1, 0, width, picked[:, 0, :])
+            else:
+                max_first(i, 1)
+            max_second(i, 0)
+            if i + 1 < R_TILES:
+                multiply(i + 1, 0)
+            if picks:
+                max_first(i, 1)
+                pick_supine(i - 1, 0, width, weighted, picked[:, 1, :], "bank6")
+            max_second(i, 1)
+            if i + 1 < R_TILES:
+                multiply(i + 1, 1)
+            if i + 2 < R_TILES:
+                prepare(i + 2)
+            if i == 1:
+                w4_codes = stage.tile([P, 2, N], U32, name="w4_codes", tag="b", align_bytes=64)
+                nc.sync.dma_start(
+                    w4_codes[:].bitcast(I32), w4_words.rearrange("a p c i -> p a (c i)").bitcast(I32)
+                )
+            if i == 4:
+                turn_back(0, 0, M, False)
+            if i == R_TILES - 2:
+                quantise_z(0, 0, M)
+
+        def second_passes(c0, cw, b):
+            codes, scales = z_quantised[(b, c0 * b)]
+            cols = slice(c0 * (1 - b), c0 * (1 - b) + cw)
+            per_bank = BANK // cw
+            for nt in range(N_TILES):
+                bank, slot = divmod(nt, per_bank)
+                nc.tensor.matmul_mx(
+                    out=y_banks[c0][bank][:, slot * cw : (slot + 1) * cw],
+                    lhsT=w4_codes[:, b, nt * P : (nt + 1) * P].bitcast(FP8X4),
+                    lhsT_scale=w4_plane[:, b, nt * P : (nt + 1) * P],
+                    rhs=codes[:, cols].bitcast(FP8X4),
+                    rhs_scale=scales[:, cols],
+                    start=(b == 0 and slot == 0),
+                    stop=(b == 1 and (slot == per_bank - 1 or nt == N_TILES - 1)),
+                )
+
+        y_banks = {}
+        taken = 0
+        for c0, cw in M_CHUNKS:
+            y_banks[c0] = []
+            for bank in range((N_TILES * cw + BANK - 1) // BANK):
+                y_banks[c0].append(psum.tile([P, BANK], F32, name="y", tag="bank%d" % taken))
+                taken = taken + 1
+            second_passes(c0, cw, 0)
+
+        def finish(c0, cw):
+            quantise_z(1, c0, cw)
+            second_passes(c0, cw, 1)
+            magnitude = held.tile([P, N_TILES * cw], F32, name="magnitude%d" % c0)
+            for bank, y in enumerate(y_banks[c0]):
+                used = min(BANK, N_TILES * cw - bank * BANK)
+                nc.scalar.activation(magnitude[:, bank * BANK : bank * BANK + used], y[:, 0:used], ACT.Abs)
+            result = held.tile([P, N_TILES, cw], F32, name="result%d" % c0)
+            for nt in range(N_TILES):
+                nc.scalar.activation(
+                    result[:, nt, :], magnitude[:, nt * cw : (nt + 1) * cw], ACT.Sqrt, bias=base_col[:, nt : nt + 1]
+                )
+            nc.sync.dma_start(out[:, c0 : c0 + cw].rearrange("(t p) m -> p t m", p=P), result[:])
+
+        c0, cw = M_CHUNKS[0]
+        picked = ring2.tile([P, 2, cw], F32, name="picked", tag="picked")
+        weighted = pick_side(R_TILES - 1, c0, cw, picked[:, 0, :])
+        pick_supine(R_TILES - 1, c0, cw, weighted, picked[:, 1, :], "bank6")
+        turn_back(1, c0, cw, False)
+        previous = (c0, cw)
+        unit = 0
+        for c0, cw in M_CHUNKS[1:]:
+            picked = ring2.tile([P, TAIL_TILES, 2, cw], F32, name="picked_late", tag="pair")
+            for k in range(TAIL_TILES):
+                i = whole_tiles + k
+                weighted = pick_side(i, c0, cw, picked[:, k, 0, :])
+                pick_supine(i, c0, cw, weighted, picked[:, k, 1, :], "bank%d" % (4 + unit % 3))
+                unit = unit + 1
+                if k == TAIL_TILES - 1:
+                    finish(*previous)
+            turn_back(1, c0, cw, c0 == M_CHUNKS[-1][0])
+            previous = (c0, cw)
+        finish(*previous)

@@ -48,55 +48,52 @@ def tile_list_sleeper_support_rating_kernel(
         v_words = [held.tile([P, BANK], U32, name="v_words%d" % half, align_bytes=64) for half in range(2)]
         w1_codes = held.tile([P, 2 * H], U8, name="w1_codes", align_bytes=64)
         w1_plane = held.tile([P, H], U8, name="w1_plane", align_bytes=64)
-        w4_plane = held.tile([P, 2, N], U8, name="w4_plane", align_bytes=64)
-        rows = held.tile([P, P], F32, name="rows")
         identity = held.tile([P, P], F32, name="identity")
         neg_side = held.tile([P, R_TILES], F32, name="neg_side")
         base_col = held.tile([P, N_TILES], F32, name="base_col")
 
         nc.gpsimd.memset(table_bytes[:].bitcast(I32), 0)
         nc.vector.memset(w1_plane[:].bitcast(I32), 0)
-        nc.vector.memset(rows[:], 0.0)
         nc.vector.memset(v_scales[:].bitcast(I32), 0)
-        nc.vector.memset(w4_plane[:].rearrange("p a n -> p (a n)").bitcast(I32), 0)
         nc.sync.dma_start(offs_t[:], offs)
         nc.sync.dma_start(pos2_t[:], pos2)
         nc.sync.dma_start(pos1_t[:], pos1)
+        nc.sync.dma_start(w1_codes[:].bitcast(I32), w1_words[0].bitcast(I32))
         nc.sync.dma_start(table_words[:].bitcast(I32), tab_words[0].rearrange("p t i -> p (t i)").bitcast(I32))
         nc.scalar.dma_start(table_bytes[0:P:8, :].bitcast(I32), tab_scales[0].bitcast(I32))
+        make_identity(nc, identity[:])
         for d in range(4):
             queue = nc.gpsimd if d < 3 else nc.scalar
             queue.dma_start(
                 w1_plane[32 * d : 32 * d + 4, :].bitcast(I32), w1_scales[0, 4 * d : 4 * d + 4, :].bitcast(I32)
             )
-        nc.sync.dma_start(w1_codes[:].bitcast(I32), w1_words[0].bitcast(I32))
+
+        warm = held.tile([P, 2], F32, name="warm")
+        nc.vector.memset(warm[:, 0:1], 1.0)
+        nc.scalar.activation(warm[:, 1:2], warm[:, 0:1], ACT.Sqrt)
 
         raw = {}
 
         def load_chunk(first, count, tag):
             cols = slice(first * P, (first + count) * P)
-            chunk = stage.tile([P, 2, 4, count * P], F32, name="chunk", tag=tag, align_bytes=64)
+            chunk = stage.tile([P, 9, count * P], F32, name="chunk", tag=tag, align_bytes=64)
             for slot, w in enumerate((w2, w3)):
-                nc.sync.dma_start(chunk[:, slot, :, :], w[:, cols].rearrange("(p j) c -> p j c", j=4))
+                part = chunk[:, 4 * slot : 4 * slot + 4, :]
+                nc.sync.dma_start(part, w[:, cols].rearrange("(p j) c -> p j c", j=4))
                 for i in range(count):
-                    raw[(slot, first + i)] = chunk[:, slot, :, i * P : (i + 1) * P]
+                    raw[(slot, first + i)] = part[:, :, i * P : (i + 1) * P]
+            return chunk[:, 8, 0:P]
 
         load_chunk(*CHUNKS[0])
-
-        make_identity(nc, identity[:])
-        nc.gpsimd.dma_start(rows[0:R_TILES, :], side.rearrange("(i p) -> i p", p=P))
-        nc.gpsimd.dma_start(rows[R_TILES : R_TILES + N_TILES, :], base.rearrange("(i p) -> i p", p=P))
-        for d in range(4):
-            nc.gpsimd.dma_start(
-                w4_plane[32 * d : 32 * d + 4, :, :].bitcast(I32),
-                w4_scales[:, 4 * d : 4 * d + 4, :].rearrange("a q n -> q a n").bitcast(I32),
-            )
 
         nc.vector.tensor_copy(picked_bytes[:], table_bytes[:].indirect(offs_t[:]))
         for r in range(4):
             queue = nc.scalar if r % 2 else nc.sync
             queue.dma_start(v_scales[r:P:32, :].bitcast(I32), picked_bytes[8 * r : P : 32, :].bitcast(I32))
-        load_chunk(*CHUNKS[1])
+        rows = load_chunk(*CHUNKS[1])
+        nc.gpsimd.memset(rows, 0.0)
+        nc.sync.dma_start(rows[0:R_TILES, :], side.rearrange("(i p) -> i p", p=P))
+        nc.sync.dma_start(rows[R_TILES : R_TILES + N_TILES, :], base.rearrange("(i p) -> i p", p=P))
         for half in range(2):
             nc.vector.tensor_copy(v_words[half][:], table_words[:].indirect(offs_t[:, 32 * half : 32 * half + 32]))
 
@@ -167,10 +164,13 @@ def tile_list_sleeper_support_rating_kernel(
                 h_tiles[i] = ring4.tile([P, S], F32, name="h", bufs=5)
             nc.vector.tensor_tensor(h_tiles[i][:, half * BANK : (half + 1) * BANK], third[:], pair[:], ALU.max)
 
-        def pick_side(i, m0, width, picked):
+        def pick_side(i, m0, width, picked, on_scalar):
             nc.vector.tensor_copy(picked, h_tiles[i][:].indirect(pos2_t[:, m0 // 16 : (m0 + width) // 16]))
             weighted = ring3.tile([P, width], F32, name="weighted", tag="weighted")
-            nc.scalar.activation(weighted[:], picked, ACT.Copy, scale=neg_side[:, i : i + 1])
+            if on_scalar:
+                nc.scalar.activation(weighted[:], picked, ACT.Copy, scale=neg_side[:, i : i + 1])
+            else:
+                nc.gpsimd.tensor_scalar(weighted[:], picked, neg_side[:, i : i + 1], 0.0, ALU.mult, ALU.add)
             return weighted
 
         z_rows = {}
@@ -230,11 +230,12 @@ def tile_list_sleeper_support_rating_kernel(
         load_chunk(*CHUNKS[2])
 
         columns = psum.tile([P, P], F32, name="columns", tag="bank6")
-        nc.tensor.transpose(columns[:], rows[:], identity[:])
+        nc.tensor.transpose(columns[:], rows, identity[:])
         nc.scalar.activation(neg_side[:], columns[:, 0:R_TILES], ACT.Copy, scale=-1.0)
         nc.scalar.copy(base_col[:], columns[:, R_TILES : R_TILES + N_TILES])
 
         w4_codes = None
+        w4_plane = None
         whole_tiles = R_TILES - TAIL_TILES
         for i in range(R_TILES):
             picks = i > 0
@@ -242,7 +243,7 @@ def tile_list_sleeper_support_rating_kernel(
             max_first(i, 0)
             if picks:
                 picked = ring2.tile([P, 2, width], F32, name="picked", tag="picked")
-                weighted = pick_side(i - 1, 0, width, picked[:, 0, :])
+                weighted = pick_side(i - 1, 0, width, picked[:, 0, :], False)
             else:
                 max_first(i, 1)
             max_second(i, 0)
@@ -261,6 +262,14 @@ def tile_list_sleeper_support_rating_kernel(
                 nc.sync.dma_start(
                     w4_codes[:].bitcast(I32), w4_words.rearrange("a p c i -> p a (c i)").bitcast(I32)
                 )
+            if i + 2 == R_TILES - 1:
+                w4_plane = stage.tile([P, 2, N], U8, name="w4_plane", tag="a", align_bytes=64)
+                nc.gpsimd.memset(w4_plane[:].rearrange("p a n -> p (a n)").bitcast(I32), 0)
+                for d in range(4):
+                    nc.sync.dma_start(
+                        w4_plane[32 * d : 32 * d + 4, :, :].bitcast(I32),
+                        w4_scales[:, 4 * d : 4 * d + 4, :].rearrange("a q n -> q a n").bitcast(I32),
+                    )
             if i == 4:
                 turn_back(0, 0, M, False)
             if i == R_TILES - 2:
@@ -307,7 +316,7 @@ def tile_list_sleeper_support_rating_kernel(
 
         c0, cw = M_CHUNKS[0]
         picked = ring2.tile([P, 2, cw], F32, name="picked", tag="picked")
-        weighted = pick_side(R_TILES - 1, c0, cw, picked[:, 0, :])
+        weighted = pick_side(R_TILES - 1, c0, cw, picked[:, 0, :], True)
         pick_supine(R_TILES - 1, c0, cw, weighted, picked[:, 1, :], "bank6")
         turn_back(1, c0, cw, False)
         previous = (c0, cw)
@@ -316,7 +325,7 @@ def tile_list_sleeper_support_rating_kernel(
             picked = ring2.tile([P, TAIL_TILES, 2, cw], F32, name="picked_late", tag="pair")
             for k in range(TAIL_TILES):
                 i = whole_tiles + k
-                weighted = pick_side(i, c0, cw, picked[:, k, 0, :])
+                weighted = pick_side(i, c0, cw, picked[:, k, 0, :], True)
                 pick_supine(i, c0, cw, weighted, picked[:, k, 1, :], "bank%d" % (4 + unit % 3))
                 unit = unit + 1
                 if k == TAIL_TILES - 1:

@@ -122,47 +122,55 @@ def tile_list_sleeper_support_rating_kernel(
 
         sums = {}
 
-        def multiply(i, half):
-            codes, scales = quantised[i]
-            moving = v_words[half][:].bitcast(FP8X4)
-            moving_scales = v_scales[:, half * BANK : (half + 1) * BANK]
-            banks = [psum.tile([P, BANK], F32, name="sums", tag="bank%d" % (2 * k + half)) for k in range(3)]
+        def multiply(i, half, k):
+            codes, scales = quantised.get(i, (None, None))
+            if k == 0:
+                weights = w1_codes[:, 2 * P * i : 2 * P * (i + 1)].bitcast(FP4X4)
+                weight_scales = w1_plane[:, P * i : P * (i + 1)]
+            else:
+                weights = codes[:, (k - 1) * P : k * P].bitcast(FP8X4)
+                weight_scales = scales[:, (k - 1) * P : k * P]
+            bank = psum.tile([P, BANK], F32, name="sums", tag="bank%d" % (2 * k + half))
             nc.tensor.matmul_mx(
-                out=banks[0][:],
-                lhsT=w1_codes[:, 2 * P * i : 2 * P * (i + 1)].bitcast(FP4X4),
-                lhsT_scale=w1_plane[:, P * i : P * (i + 1)],
-                rhs=moving,
-                rhs_scale=moving_scales,
+                out=bank[:],
+                lhsT=weights,
+                lhsT_scale=weight_scales,
+                rhs=v_words[half][:].bitcast(FP8X4),
+                rhs_scale=v_scales[:, half * BANK : (half + 1) * BANK],
                 start=True,
                 stop=True,
             )
-            for slot in range(2):
-                nc.tensor.matmul_mx(
-                    out=banks[1 + slot][:],
-                    lhsT=codes[:, slot * P : (slot + 1) * P].bitcast(FP8X4),
-                    lhsT_scale=scales[:, slot * P : (slot + 1) * P],
-                    rhs=moving,
-                    rhs_scale=moving_scales,
-                    start=True,
-                    stop=True,
-                )
-            first = ring3.tile([P, BANK], F32, name="first")
-            nc.scalar.copy(first[:], banks[0][:])
-            sums[(i, half)] = (first, banks[1], banks[2])
+            if k == 0:
+                first = ring4.tile([P, BANK], F32, name="first")
+                nc.scalar.copy(first[:], bank[:])
+                sums[(i, half, k)] = first
+            else:
+                sums[(i, half, k)] = bank
+
+        pairs = {}
 
         def max_first(i, half):
-            first, second, third = sums[(i, half)]
             pair = ring2.tile([P, BANK], F32, name="pair", tag="pair")
-            nc.vector.tensor_tensor(pair[:], second[:], first[:], ALU.max)
-            sums[(i, half)] = (pair, third)
+            nc.vector.tensor_tensor(pair[:], sums[(i, half, 1)][:], sums[(i, half, 0)][:], ALU.max)
+            pairs[(i, half)] = pair
+            if i + 1 < R_TILES:
+                multiply(i + 1, half, 1)
 
         h_tiles = {}
 
         def max_second(i, half):
-            pair, third = sums[(i, half)]
             if half == 0:
                 h_tiles[i] = ring4.tile([P, S], F32, name="h", bufs=5)
-            nc.vector.tensor_tensor(h_tiles[i][:, half * BANK : (half + 1) * BANK], third[:], pair[:], ALU.max)
+            nc.vector.tensor_tensor(
+                h_tiles[i][:, half * BANK : (half + 1) * BANK], sums[(i, half, 2)][:], pairs[(i, half)][:], ALU.max
+            )
+            if i == 0 and half == 0:
+                columns = psum.tile([P, P], F32, name="columns", tag="bank4")
+                nc.tensor.transpose(columns[:], rows, identity[:])
+                nc.scalar.activation(neg_side[:], columns[:, 0:R_TILES], ACT.Copy, scale=-1.0)
+                nc.scalar.copy(base_col[:], columns[:, R_TILES : R_TILES + N_TILES])
+            if i + 1 < R_TILES:
+                multiply(i + 1, half, 2)
 
         def pick_side(i, m0, width, picked, on_scalar):
             nc.vector.tensor_copy(picked, h_tiles[i][:].indirect(pos2_t[:, m0 // 16 : (m0 + width) // 16]))
@@ -224,37 +232,29 @@ def tile_list_sleeper_support_rating_kernel(
             z_quantised[(b, c0)] = (codes, scales)
 
         prepare(0)
-        multiply(0, 0)
-        multiply(0, 1)
+        for half in range(2):
+            for k in range(3):
+                multiply(0, half, k)
         prepare(1)
         load_chunk(*CHUNKS[2])
-
-        columns = psum.tile([P, P], F32, name="columns", tag="bank6")
-        nc.tensor.transpose(columns[:], rows, identity[:])
-        nc.scalar.activation(neg_side[:], columns[:, 0:R_TILES], ACT.Copy, scale=-1.0)
-        nc.scalar.copy(base_col[:], columns[:, R_TILES : R_TILES + N_TILES])
 
         w4_codes = None
         w4_plane = None
         whole_tiles = R_TILES - TAIL_TILES
         for i in range(R_TILES):
-            picks = i > 0
             width = M if i <= whole_tiles else M_CHUNKS[0][1]
-            max_first(i, 0)
-            if picks:
+            if i + 1 < R_TILES:
+                for half in range(2):
+                    multiply(i + 1, half, 0)
+            if i > 0:
                 picked = ring2.tile([P, 2, width], F32, name="picked", tag="picked")
                 weighted = pick_side(i - 1, 0, width, picked[:, 0, :], False)
-            else:
-                max_first(i, 1)
-            max_second(i, 0)
-            if i + 1 < R_TILES:
-                multiply(i + 1, 0)
-            if picks:
-                max_first(i, 1)
+            for half in range(2):
+                max_first(i, half)
+            if i > 0:
                 pick_supine(i - 1, 0, width, weighted, picked[:, 1, :], "bank6")
-            max_second(i, 1)
-            if i + 1 < R_TILES:
-                multiply(i + 1, 1)
+            for half in range(2):
+                max_second(i, half)
             if i + 2 < R_TILES:
                 prepare(i + 2)
             if i == 1:
@@ -278,7 +278,7 @@ def tile_list_sleeper_support_rating_kernel(
         def second_passes(c0, cw, b):
             codes, scales = z_quantised[(b, c0 * b)]
             cols = slice(c0 * (1 - b), c0 * (1 - b) + cw)
-            per_bank = BANK // cw
+            per_bank = -(-N_TILES // len(y_banks[c0]))
             for nt in range(N_TILES):
                 bank, slot = divmod(nt, per_bank)
                 nc.tensor.matmul_mx(
@@ -292,28 +292,31 @@ def tile_list_sleeper_support_rating_kernel(
                 )
 
         y_banks = {}
-        taken = 0
-        for c0, cw in M_CHUNKS:
-            y_banks[c0] = []
-            for bank in range((N_TILES * cw + BANK - 1) // BANK):
-                y_banks[c0].append(psum.tile([P, BANK], F32, name="y", tag="bank%d" % taken))
-                taken = taken + 1
+
+        def open_sums(c0, cw, numbers):
+            y_banks[c0] = [psum.tile([P, BANK], F32, name="y", tag="bank%d" % n) for n in numbers]
             second_passes(c0, cw, 0)
 
         def finish(c0, cw):
             quantise_z(1, c0, cw)
             second_passes(c0, cw, 1)
             magnitude = held.tile([P, N_TILES * cw], F32, name="magnitude%d" % c0)
-            for bank, y in enumerate(y_banks[c0]):
-                used = min(BANK, N_TILES * cw - bank * BANK)
-                nc.scalar.activation(magnitude[:, bank * BANK : bank * BANK + used], y[:, 0:used], ACT.Abs)
             result = held.tile([P, N_TILES, cw], F32, name="result%d" % c0)
+            per_bank = -(-N_TILES // len(y_banks[c0]))
+            for bank, y in enumerate(y_banks[c0]):
+                lo, hi = bank * per_bank, min(N_TILES, (bank + 1) * per_bank)
+                nc.scalar.activation(magnitude[:, lo * cw : hi * cw], y[:, 0 : (hi - lo) * cw], ACT.Abs)
             for nt in range(N_TILES):
                 nc.scalar.activation(
                     result[:, nt, :], magnitude[:, nt * cw : (nt + 1) * cw], ACT.Sqrt, bias=base_col[:, nt : nt + 1]
                 )
-            nc.sync.dma_start(out[:, c0 : c0 + cw].rearrange("(t p) m -> p t m", p=P), result[:])
+                if per_bank == 1:
+                    nc.sync.dma_start(out[nt * P : (nt + 1) * P, c0 : c0 + cw], result[:, nt, :])
+            if per_bank > 1:
+                nc.sync.dma_start(out[:, c0 : c0 + cw].rearrange("(t p) m -> p t m", p=P), result[:])
 
+        open_sums(*M_CHUNKS[0], (0, 1))
+        open_sums(*M_CHUNKS[1], (2,))
         c0, cw = M_CHUNKS[0]
         picked = ring2.tile([P, 2, cw], F32, name="picked", tag="picked")
         weighted = pick_side(R_TILES - 1, c0, cw, picked[:, 0, :], True)
@@ -330,6 +333,8 @@ def tile_list_sleeper_support_rating_kernel(
                 unit = unit + 1
                 if k == TAIL_TILES - 1:
                     finish(*previous)
+                    if previous == M_CHUNKS[0]:
+                        open_sums(*M_CHUNKS[2], (3, 0, 1))
             turn_back(1, c0, cw, c0 == M_CHUNKS[-1][0])
             previous = (c0, cw)
         finish(*previous)

@@ -41,36 +41,38 @@ def tile_list_sleeper_support_rating_kernel(
         offs_t = held.tile([P, S // 16], U16, name="offs_t")
         pos1_t = held.tile([P, M // 16], U16, name="pos1_t")
         pos2_t = held.tile([P, M // 16], U16, name="pos2_t")
-        table_words = held.tile([P, T], U32, name="table_words", align_bytes=64)
         table_bytes = stage.tile([P, T], U8, name="table_bytes", tag="b", align_bytes=64)
         picked_bytes = held.tile([P, S], U8, name="picked_bytes", align_bytes=64)
         v_scales = held.tile([P, S], U8, name="v_scales", align_bytes=64)
         v_words = [held.tile([P, BANK], U32, name="v_words%d" % half, align_bytes=64) for half in range(2)]
-        w1_codes = held.tile([P, 2 * H], U8, name="w1_codes", align_bytes=64)
         w1_plane = held.tile([P, H], U8, name="w1_plane", align_bytes=64)
         identity = held.tile([P, P], F32, name="identity")
         neg_side = held.tile([P, R_TILES], F32, name="neg_side")
         base_col = held.tile([P, N_TILES], F32, name="base_col")
 
         nc.gpsimd.memset(table_bytes[:].bitcast(I32), 0)
+        zeros = stage.tile([P, P], F32, name="zeros", tag="d", align_bytes=64)
+        nc.vector.memset(zeros[:], 0.0)
+        nc.vector.tensor_copy(identity[:], zeros[:])
         nc.vector.memset(w1_plane[:].bitcast(I32), 0)
         nc.vector.memset(v_scales[:].bitcast(I32), 0)
         nc.sync.dma_start(offs_t[:], offs)
         nc.sync.dma_start(pos2_t[:], pos2)
         nc.sync.dma_start(pos1_t[:], pos1)
-        nc.sync.dma_start(w1_codes[:].bitcast(I32), w1_words[0].bitcast(I32))
+        table_words = stage.tile([P, T], U32, name="table_words", tag="d", align_bytes=64)
         nc.sync.dma_start(table_words[:].bitcast(I32), tab_words[0].rearrange("p t i -> p (t i)").bitcast(I32))
         nc.scalar.dma_start(table_bytes[0:P:8, :].bitcast(I32), tab_scales[0].bitcast(I32))
-        make_identity(nc, identity[:])
+        make_identity(nc, identity[:], nomemset=True)
         for d in range(4):
             queue = nc.gpsimd if d < 3 else nc.scalar
             queue.dma_start(
                 w1_plane[32 * d : 32 * d + 4, :].bitcast(I32), w1_scales[0, 4 * d : 4 * d + 4, :].bitcast(I32)
             )
 
-        warm = held.tile([P, 2], F32, name="warm")
-        nc.vector.memset(warm[:, 0:1], 1.0)
-        nc.scalar.activation(warm[:, 1:2], warm[:, 0:1], ACT.Sqrt)
+        warm_in = stage.tile([P, 1], F32, name="warm_in", tag="a", align_bytes=64)
+        warm_out = stage.tile([P, 1], F32, name="warm_out", tag="c", align_bytes=64)
+        nc.vector.memset(warm_in[:], 1.0)
+        nc.scalar.activation(warm_out[:], warm_in[:], ACT.Sqrt)
 
         raw = {}
 
@@ -85,6 +87,8 @@ def tile_list_sleeper_support_rating_kernel(
             return chunk[:, 8, 0:P]
 
         load_chunk(*CHUNKS[0])
+        w1_codes = stage.tile([P, 2 * H], U8, name="w1_codes", tag="c", align_bytes=64)
+        nc.sync.dma_start(w1_codes[:].bitcast(I32), w1_words[0].bitcast(I32))
 
         nc.vector.tensor_copy(picked_bytes[:], table_bytes[:].indirect(offs_t[:]))
         for r in range(4):
@@ -123,13 +127,13 @@ def tile_list_sleeper_support_rating_kernel(
         sums = {}
 
         def multiply(i, half, k):
-            codes, scales = quantised.get(i, (None, None))
-            if k == 0:
+            codes, scales = quantised[i]
+            if k == 1:
                 weights = w1_codes[:, 2 * P * i : 2 * P * (i + 1)].bitcast(FP4X4)
                 weight_scales = w1_plane[:, P * i : P * (i + 1)]
             else:
-                weights = codes[:, (k - 1) * P : k * P].bitcast(FP8X4)
-                weight_scales = scales[:, (k - 1) * P : k * P]
+                weights = codes[:, (k // 2) * P : (k // 2 + 1) * P].bitcast(FP8X4)
+                weight_scales = scales[:, (k // 2) * P : (k // 2 + 1) * P]
             bank = psum.tile([P, BANK], F32, name="sums", tag="bank%d" % (2 * k + half))
             nc.tensor.matmul_mx(
                 out=bank[:],
@@ -183,7 +187,7 @@ def tile_list_sleeper_support_rating_kernel(
 
         z_rows = {}
 
-        def pick_supine(i, m0, width, weighted, picked, bank):
+        def pick_supine(i, m0, width, weighted, picked, bank, on_vector=False):
             nc.vector.tensor_copy(picked, h_tiles[i][:].indirect(pos1_t[:, m0 // 16 : (m0 + width) // 16]))
             blocks = width // P
             turned = psum.tile([P, blocks, P], F32, name="turned", tag=bank)
@@ -198,7 +202,8 @@ def tile_list_sleeper_support_rating_kernel(
             b, quarter = divmod(i, 4)
             if (b, m0) not in z_rows:
                 z_rows[(b, m0)] = held.tile([P, blocks, 2, 2 * P], BF16, name="z_rows%d_%d" % (b, m0), align_bytes=64)
-            nc.scalar.copy(
+            copy = nc.vector.tensor_copy if on_vector else nc.scalar.copy
+            copy(
                 z_rows[(b, m0)][:, :, :, 64 * quarter : 64 * (quarter + 1)].rearrange("m t u (q e) -> m t u q e", e=2),
                 turned[:].rearrange("m t (q u e) -> m t u q e", u=2, e=2),
             )
@@ -326,10 +331,14 @@ def tile_list_sleeper_support_rating_kernel(
         unit = 0
         for c0, cw in M_CHUNKS[1:]:
             picked = ring2.tile([P, TAIL_TILES, 2, cw], F32, name="picked_late", tag="pair")
+            ahead = pick_side(whole_tiles, c0, cw, picked[:, 0, 0, :], True)
             for k in range(TAIL_TILES):
                 i = whole_tiles + k
-                weighted = pick_side(i, c0, cw, picked[:, k, 0, :], True)
-                pick_supine(i, c0, cw, weighted, picked[:, k, 1, :], "bank%d" % (4 + unit % 3))
+                weighted = ahead
+                if k + 1 < TAIL_TILES:
+                    ahead = pick_side(i + 1, c0, cw, picked[:, k + 1, 0, :], True)
+                closing = c0 == M_CHUNKS[-1][0] and k == TAIL_TILES - 1
+                pick_supine(i, c0, cw, weighted, picked[:, k, 1, :], "bank%d" % (4 + unit % 3), closing)
                 unit = unit + 1
                 if k == TAIL_TILES - 1:
                     finish(*previous)

from contextlib import ExitStack

import concourse.mybir as mybir
from concourse.masks import make_identity

K, T, S, M, H, N = 512, 2048, 1024, 512, 1024, 384
FLOPS = 2 * (3 * K * H * S + H * N * M)

F32 = mybir.dt.float32
BF16 = mybir.dt.bfloat16
I32 = mybir.dt.int32
U32 = mybir.dt.uint32
U16 = mybir.dt.uint16
U8 = mybir.dt.uint8
FP8X4 = mybir.dt.float8_e4m3fn_x4
FP4X4 = mybir.dt.float4_e2m1fn_x4
ALU = mybir.AluOpType
ACT = mybir.ActivationFunctionType

P = 128
BANK = 512
R_TILES = H // P
N_TILES = N // P
TAIL_TILES = 4
M_CHUNKS = ((0, 256), (256, 128), (384, 128))
CHUNKS = ((0, 2, "a"), (2, 2, "b"), (4, 4, "a"))


def tile_list_sleeper_support_rating_kernel(
    tc, tab_words, tab_scales, offs, pos1, pos2, w1_words, w1_scales, w2, w3, w4_words, w4_scales, side, base, out
):
    nc = tc.nc
    with ExitStack() as ctx:
        held = ctx.enter_context(tc.tile_pool(name="held", bufs=1))
        stage = ctx.enter_context(tc.tile_pool(name="stage", bufs=1))
        ring2 = ctx.enter_context(tc.tile_pool(name="ring2", bufs=2))
        ring3 = ctx.enter_context(tc.tile_pool(name="ring3", bufs=3))
        ring4 = ctx.enter_context(tc.tile_pool(name="ring4", bufs=4))
        psum = ctx.enter_context(tc.psum_pool(name="psum", bufs=1))

        offs_t = held.tile([P, S // 16], U16, name="offs_t")
        pos1_t = held.tile([P, M // 16], U16, name="pos1_t")
        pos2_t = held.tile([P, M // 16], U16, name="pos2_t")
        table_bytes = stage.tile([P, T], U8, name="table_bytes", tag="b", align_bytes=64)
        picked_bytes = held.tile([P, S], U8, name="picked_bytes", align_bytes=64)
        v_scales = held.tile([P, S], U8, name="v_scales", align_bytes=64)
        v_words = [held.tile([P, BANK], U32, name="v_words%d" % half, align_bytes=64) for half in range(2)]
        w1_plane = held.tile([P, H], U8, name="w1_plane", align_bytes=64)
        identity = held.tile([P, P], F32, name="identity")
        neg_side = held.tile([P, R_TILES], F32, name="neg_side")
        base_col = held.tile([P, N_TILES], F32, name="base_col")

        nc.gpsimd.memset(table_bytes[:].bitcast(I32), 0)
        zeros = stage.tile([P, P], F32, name="zeros", tag="d", align_bytes=64)
        nc.vector.memset(zeros[:], 0.0)
        nc.vector.tensor_copy(identity[:], zeros[:])
        nc.vector.memset(w1_plane[:].bitcast(I32), 0)
        nc.vector.memset(v_scales[:].bitcast(I32), 0)
        nc.sync.dma_start(offs_t[:], offs)
        nc.sync.dma_start(pos2_t[:], pos2)
        nc.sync.dma_start(pos1_t[:], pos1)
        table_words = stage.tile([P, T], U32, name="table_words", tag="d", align_bytes=64)
        nc.sync.dma_start(table_words[:].bitcast(I32), tab_words[0].rearrange("p t i -> p (t i)").bitcast(I32))
        nc.scalar.dma_start(table_bytes[0:P:8, :].bitcast(I32), tab_scales[0].bitcast(I32))
        make_identity(nc, identity[:], nomemset=True)
        for d in range(4):
            queue = nc.gpsimd if d < 3 else nc.scalar
            queue.dma_start(
                w1_plane[32 * d : 32 * d + 4, :].bitcast(I32), w1_scales[0, 4 * d : 4 * d + 4, :].bitcast(I32)
            )

        warm_in = stage.tile([P, 1], F32, name="warm_in", tag="a", align_bytes=64)
        warm_out = stage.tile([P, 1], F32, name="warm_out", tag="c", align_bytes=64)
        nc.vector.memset(warm_in[:], 1.0)
        nc.scalar.activation(warm_out[:], warm_in[:], ACT.Sqrt)

        raw = {}

        def load_chunk(first, count, tag):
            cols = slice(first * P, (first + count) * P)
            chunk = stage.tile([P, 9, count * P], F32, name="chunk", tag=tag, align_bytes=64)
            for slot, w in enumerate((w2, w3)):
                part = chunk[:, 4 * slot : 4 * slot + 4, :]
                nc.sync.dma_start(part, w[:, cols].rearrange("(p j) c -> p j c", j=4))
                for i in range(count):
                    raw[(slot, first + i)] = part[:, :, i * P : (i + 1) * P]
            return chunk[:, 8, 0:P]

        load_chunk(*CHUNKS[0])
        w1_codes = stage.tile([P, 2 * H], U8, name="w1_codes", tag="c", align_bytes=64)
        nc.sync.dma_start(w1_codes[:].bitcast(I32), w1_words[0].bitcast(I32))

        nc.vector.tensor_copy(picked_bytes[:], table_bytes[:].indirect(offs_t[:]))
        for r in range(4):
            queue = nc.scalar if r % 2 else nc.sync
            queue.dma_start(v_scales[r:P:32, :].bitcast(I32), picked_bytes[8 * r : P : 32, :].bitcast(I32))
        rows = load_chunk(*CHUNKS[1])
        nc.gpsimd.memset(rows, 0.0)
        nc.sync.dma_start(rows[0:R_TILES, :], side.rearrange("(i p) -> i p", p=P))
        nc.sync.dma_start(rows[R_TILES : R_TILES + N_TILES, :], base.rearrange("(i p) -> i p", p=P))
        for half in range(2):
            nc.vector.tensor_copy(v_words[half][:], table_words[:].indirect(offs_t[:, 32 * half : 32 * half + 32]))

        quantised = {}

        def prepare(i):
            grouped = ring2.tile([P, 2, P, 4], BF16, name="grouped", align_bytes=64)
            for slot in range(2):
                nc.scalar.copy(
                    grouped[:, slot, :, :].rearrange("p (c i) t -> p c t i", i=4),
                    raw[(slot, i)].rearrange("p t (c i) -> p c t i", i=4),
                )
            codes = ring3.tile([P, 2 * P], U32, name="w_codes", align_bytes=64)
            scales = ring3.tile([P, 2 * P], U8, name="w_scales", align_bytes=64)
            parts = 2 if i == 0 else 1
            width = 2 * P // parts
            flat = grouped[:].rearrange("p s c t -> p (s c t)")
            for part in range(parts):
                cols = slice(part * width, (part + 1) * width)
                nc.vector.quantize_mx(
                    out=codes[:, cols].bitcast(FP8X4),
                    scales=scales[:, cols],
                    in_=flat[:, 4 * part * width : 4 * (part + 1) * width],
                )
            quantised[i] = (codes, scales)

        sums = {}

        def multiply(i, half, k):
            codes, scales = quantised[i]
            if k == 1:
                weights = w1_codes[:, 2 * P * i : 2 * P * (i + 1)].bitcast(FP4X4)
                weight_scales = w1_plane[:, P * i : P * (i + 1)]
            else:
                weights = codes[:, (k // 2) * P : (k // 2 + 1) * P].bitcast(FP8X4)
                weight_scales = scales[:, (k // 2) * P : (k // 2 + 1) * P]
            bank = psum.tile([P, BANK], F32, name="sums", tag="bank%d" % (2 * k + half))
            nc.tensor.matmul_mx(
                out=bank[:],
                lhsT=weights,
                lhsT_scale=weight_scales,
                rhs=v_words[half][:].bitcast(FP8X4),
                rhs_scale=v_scales[:, half * BANK : (half + 1) * BANK],
                start=True,
                stop=True,
            )
            if k == 0:
                first = ring4.tile([P, BANK], F32, name="first")
                nc.scalar.copy(first[:], bank[:])
                sums[(i, half, k)] = first
            else:
                sums[(i, half, k)] = bank

        pairs = {}

        def max_first(i, half):
            pair = ring2.tile([P, BANK], F32, name="pair", tag="pair")
            nc.vector.tensor_tensor(pair[:], sums[(i, half, 1)][:], sums[(i, half, 0)][:], ALU.max)
            pairs[(i, half)] = pair
            if i + 1 < R_TILES:
                multiply(i + 1, half, 1)

        h_tiles = {}

        def max_second(i, half):
            if half == 0:
                h_tiles[i] = ring4.tile([P, S], F32, name="h", bufs=5)
            nc.vector.tensor_tensor(
                h_tiles[i][:, half * BANK : (half + 1) * BANK], sums[(i, half, 2)][:], pairs[(i, half)][:], ALU.max
            )
            if i == 0 and half == 0:
                columns = psum.tile([P, P], F32, name="columns", tag="bank4")
                nc.tensor.transpose(columns[:], rows, identity[:])
                nc.scalar.activation(neg_side[:], columns[:, 0:R_TILES], ACT.Copy, scale=-1.0)
                nc.scalar.copy(base_col[:], columns[:, R_TILES : R_TILES + N_TILES])
            if i + 1 < R_TILES:
                multiply(i + 1, half, 2)

        def pick_side(i, m0, width, picked, on_scalar):
            nc.vector.tensor_copy(picked, h_tiles[i][:].indirect(pos2_t[:, m0 // 16 : (m0 + width) // 16]))
            weighted = ring3.tile([P, width], F32, name="weighted", tag="weighted")
            if on_scalar:
                nc.scalar.activation(weighted[:], picked, ACT.Copy, scale=neg_side[:, i : i + 1])
            else:
                nc.gpsimd.tensor_scalar(weighted[:], picked, neg_side[:, i : i + 1], 0.0, ALU.mult, ALU.add)
            return weighted

        z_rows = {}

        def pick_supine(i, m0, width, weighted, picked, bank, on_vector=False):
            nc.vector.tensor_copy(picked, h_tiles[i][:].indirect(pos1_t[:, m0 // 16 : (m0 + width) // 16]))
            blocks = width // P
            turned = psum.tile([P, blocks, P], F32, name="turned", tag=bank)
            for mt in range(blocks):
                cols = slice(mt * P, (mt + 1) * P)
                nc.tensor.matmul(
                    turned[:, mt, :], weighted[:, cols], identity[:], start=True, stop=False, is_transpose=True
                )
                nc.tensor.matmul(
                    turned[:, mt, :], picked[:, cols], identity[:], start=False, stop=True, is_transpose=True
                )
            b, quarter = divmod(i, 4)
            if (b, m0) not in z_rows:
                z_rows[(b, m0)] = held.tile([P, blocks, 2, 2 * P], BF16, name="z_rows%d_%d" % (b, m0), align_bytes=64)
            copy = nc.vector.tensor_copy if on_vector else nc.scalar.copy
            copy(
                z_rows[(b, m0)][:, :, :, 64 * quarter : 64 * (quarter + 1)].rearrange("m t u (q e) -> m t u q e", e=2),
                turned[:].rearrange("m t (q u e) -> m t u q e", u=2, e=2),
            )

        z_quantised = {}

        def turn_back(b, c0, cw, on_vector):
            words = z_rows[(b, c0)][:].rearrange("m t u w -> m (t u w)").bitcast(F32)
            grouped = held.tile([P, cw * 4], BF16, name="z_grouped%d_%d" % (b, c0), align_bytes=64)
            blocks = min(2, cw // P)
            for first_block in range(0, cw // P, blocks):
                back = psum.tile([P, blocks, 2, P], F32, name="back", tag="bank7")
                for mt in range(blocks):
                    for u in range(2):
                        at = (2 * (first_block + mt) + u) * P
                        nc.tensor.transpose(back[:, mt, u, :], words[:, at : at + P], identity[:])
                target = grouped[:, 4 * P * first_block : 4 * P * (first_block + blocks)].bitcast(F32)
                target = target.rearrange("p (t m u) -> p t m u", t=blocks, u=2)
                source = back[:].rearrange("p t u m -> p t m u")
                if on_vector:
                    nc.vector.tensor_copy(target, source)
                else:
                    nc.scalar.copy(target, source)
            z_quantised[(b, c0)] = grouped

        def quantise_z(b, c0, cw):
            grouped = z_quantised[(b, c0)]
            codes = held.tile([P, cw], U32, name="z_codes%d_%d" % (b, c0), align_bytes=64)
            scales = held.tile([P, cw], U8, name="z_scales%d_%d" % (b, c0), align_bytes=64)
            nc.vector.quantize_mx(out=codes[:].bitcast(FP8X4), scales=scales[:], in_=grouped[:])
            z_quantised[(b, c0)] = (codes, scales)

        prepare(0)
        for half in range(2):
            for k in range(3):
                multiply(0, half, k)
        prepare(1)
        load_chunk(*CHUNKS[2])

        w4_codes = None
        w4_plane = None
        whole_tiles = R_TILES - TAIL_TILES
        for i in range(R_TILES):
            width = M if i <= whole_tiles else M_CHUNKS[0][1]
            if i + 1 < R_TILES:
                for half in range(2):
                    multiply(i + 1, half, 0)
            if i > 0:
                picked = ring2.tile([P, 2, width], F32, name="picked", tag="picked")
                weighted = pick_side(i - 1, 0, width, picked[:, 0, :], False)
            for half in range(2):
                max_first(i, half)
            if i > 0:
                pick_supine(i - 1, 0, width, weighted, picked[:, 1, :], "bank6")
            for half in range(2):
                max_second(i, half)
            if i + 2 < R_TILES:
                prepare(i + 2)
            if i == 1:
                w4_codes = stage.tile([P, 2, N], U32, name="w4_codes", tag="b", align_bytes=64)
                nc.sync.dma_start(
                    w4_codes[:].bitcast(I32), w4_words.rearrange("a p c i -> p a (c i)").bitcast(I32)
                )
            if i + 2 == R_TILES - 1:
                w4_plane = stage.tile([P, 2, N], U8, name="w4_plane", tag="a", align_bytes=64)
                nc.gpsimd.memset(w4_plane[:].rearrange("p a n -> p (a n)").bitcast(I32), 0)
                for d in range(4):
                    nc.sync.dma_start(
                        w4_plane[32 * d : 32 * d + 4, :, :].bitcast(I32),
                        w4_scales[:, 4 * d : 4 * d + 4, :].rearrange("a q n -> q a n").bitcast(I32),
                    )
            if i == 4:
                turn_back(0, 0, M, False)
            if i == R_TILES - 2:
                quantise_z(0, 0, M)

        def second_passes(c0, cw, b):
            codes, scales = z_quantised[(b, c0 * b)]
            cols = slice(c0 * (1 - b), c0 * (1 - b) + cw)
            per_bank = -(-N_TILES // len(y_banks[c0]))
            for nt in range(N_TILES):
                bank, slot = divmod(nt, per_bank)
                nc.tensor.matmul_mx(
                    out=y_banks[c0][bank][:, slot * cw : (slot + 1) * cw],
                    lhsT=w4_codes[:, b, nt * P : (nt + 1) * P].bitcast(FP8X4),
                    lhsT_scale=w4_plane[:, b, nt * P : (nt + 1) * P],
                    rhs=codes[:, cols].bitcast(FP8X4),
                    rhs_scale=scales[:, cols],
                    start=(b == 0 and slot == 0),
                    stop=(b == 1 and (slot == per_bank - 1 or nt == N_TILES - 1)),
                )

        y_banks = {}

        def open_sums(c0, cw, numbers):
            y_banks[c0] = [psum.tile([P, BANK], F32, name="y", tag="bank%d" % n) for n in numbers]
            second_passes(c0, cw, 0)

        def finish(c0, cw):
            quantise_z(1, c0, cw)
            second_passes(c0, cw, 1)
            magnitude = held.tile([P, N_TILES * cw], F32, name="magnitude%d" % c0)
            result = held.tile([P, N_TILES, cw], F32, name="result%d" % c0)
            per_bank = -(-N_TILES // len(y_banks[c0]))
            for bank, y in enumerate(y_banks[c0]):
                lo, hi = bank * per_bank, min(N_TILES, (bank + 1) * per_bank)
                nc.scalar.activation(magnitude[:, lo * cw : hi * cw], y[:, 0 : (hi - lo) * cw], ACT.Abs)
            for nt in range(N_TILES):
                nc.scalar.activation(
                    result[:, nt, :], magnitude[:, nt * cw : (nt + 1) * cw], ACT.Sqrt, bias=base_col[:, nt : nt + 1]
                )
                if per_bank == 1:
                    nc.sync.dma_start(out[nt * P : (nt + 1) * P, c0 : c0 + cw], result[:, nt, :])
            if per_bank > 1:
                nc.sync.dma_start(out[:, c0 : c0 + cw].rearrange("(t p) m -> p t m", p=P), result[:])

        open_sums(*M_CHUNKS[0], (0, 1))
        open_sums(*M_CHUNKS[1], (2,))
        c0, cw = M_CHUNKS[0]
        picked = ring2.tile([P, 2, cw], F32, name="picked", tag="picked")
        weighted = pick_side(R_TILES - 1, c0, cw, picked[:, 0, :], True)
        pick_supine(R_TILES - 1, c0, cw, weighted, picked[:, 1, :], "bank6")
        turn_back(1, c0, cw, False)
        previous = (c0, cw)
        unit = 0
        for c0, cw in M_CHUNKS[1:]:
            picked = ring2.tile([P, TAIL_TILES, 2, cw], F32, name="picked_late", tag="pair")
            ahead = pick_side(whole_tiles, c0, cw, picked[:, 0, 0, :], True)
            for k in range(TAIL_TILES):
                i = whole_tiles + k
                weighted = ahead
                if k + 1 < TAIL_TILES:
                    ahead = pick_side(i + 1, c0, cw, picked[:, k + 1, 0, :], True)
                closing = c0 == M_CHUNKS[-1][0] and k == TAIL_TILES - 1
                pick_supine(i, c0, cw, weighted, picked[:, k, 1, :], "bank%d" % (4 + unit % 3), closing)
                unit = unit + 1
                if k == TAIL_TILES - 1:
                    finish(*previous)
                    if previous == M_CHUNKS[0]:
                        open_sums(*M_CHUNKS[2], (3, 0, 1))
            turn_back(1, c0, cw, c0 == M_CHUNKS[-1][0])
            previous = (c0, cw)
        finish(*previous)
